import numpy as np
import ml_dtypes


def mxq(x, axis, fmt="e4m3"):
    dtype, down = {"e4m3": (ml_dtypes.float8_e4m3fn, 7), "e5m2": (ml_dtypes.float8_e5m2, 14)}[fmt]
    v = np.moveaxis(np.asarray(x, np.float32).astype(ml_dtypes.bfloat16).astype(np.float64), axis, -1)
    blocks = v.reshape(v.shape[:-1] + (-1, 32))
    amax = np.abs(blocks).max(-1, keepdims=True)
    byte = np.maximum(np.where(amax > 0, np.frexp(amax)[1] - 1 + 127, 0) - down, 1)
    scale = np.exp2(byte - 127.0)
    codes = (blocks / scale).astype(np.float32).astype(dtype).astype(np.float64)
    return np.moveaxis((codes * scale).reshape(v.shape), -1, axis)


WIDE = False


def mx_kscale(k):
    if not WIDE:
        return np.ones(k)
    levels = np.array([10, -10, 5, -5, 0])
    if k % 512:
        return np.exp2(np.random.permutation(np.resize(levels, k // 32))).repeat(32)
    a = np.empty((k // 512, 16))
    for p in range(k // 512):
        a[p, :8] = np.random.permutation(np.resize(levels, 8))
        for g in range(8):
            far = levels[np.abs(levels - a[p, g]) >= 10]
            a[p, g + 8] = far[np.random.randint(len(far))]
    return np.exp2(a.ravel()).repeat(32)


def f64(x):
    return np.asarray(x).astype(np.float64)


def striped(idx):
    return np.tile(idx.reshape(-1, 16).T, (8, 1)).astype(np.uint16)


def unstriped(offs):
    return offs[:16].T.reshape(-1).astype(np.int64)


def pack_weight(w):
    k, n = w.shape
    w = f64(np.asarray(w, np.float32).astype(ml_dtypes.bfloat16)).reshape(k // 32, 32, n)
    amax = np.abs(w).max(1)
    byte = np.clip(np.where(amax > 0, np.frexp(amax)[1] - 1 + 127 - 7, 1), 1, 254)
    scaled = (w * np.exp2(127.0 - byte)[:, None, :]).reshape(k, n).astype(np.float32)
    words = np.ascontiguousarray(scaled.reshape(k // 512, 128, 4, n).transpose(0, 1, 3, 2)).astype(ml_dtypes.float8_e4m3fn).view(np.uint8)
    return words, np.ascontiguousarray(byte.astype(np.uint8).reshape(k // 512, 16, n))


def unpack_weight(words, scales):
    g, p, n, _ = words.shape
    vals = np.ascontiguousarray(words).view(ml_dtypes.float8_e4m3fn).astype(np.float64) * np.repeat(np.exp2(scales.astype(np.float64) - 127.0), 8, axis=1)[..., None]
    return vals.transpose(0, 1, 3, 2).reshape(g * 512, n)


K, T, S, N = 1024, 1024, 512, 128


def setup_inputs():
    n = np.random.standard_normal
    s = mx_kscale(K)[:, None]
    packed_xT = pack_weight(n((K, T)) * s)
    return {
        "x_words": packed_xT[0],
        "x_scales": packed_xT[1],
        "w1": (n((K, N)) / np.sqrt(K) / s).astype(np.float32),
        "guide": (n((N, S))).astype(np.float32),
        "reg": (np.random.uniform(0.1, 0.6, (N, 1))).astype(np.float32),
        "offs": striped(np.random.permutation(T)[:S]),
        "wa": striped(np.random.permutation(S)),
        "wb": striped(np.random.permutation(S)),
        "wc": striped(np.random.permutation(S)),
    }


def reference(x_words, x_scales, w1, guide, reg, offs, wa, wb, wc):
    xq = unpack_weight(x_words, x_scales)[:, unstriped(offs)]
    y = mxq(f64(w1), 0, "e4m3").T @ xq
    gy = f64(guide) * y
    mgy = (gy + gy[:, unstriped(wa)] + gy[:, unstriped(wb)]) / 3
    mg = (f64(guide) + f64(guide)[:, unstriped(wa)] + f64(guide)[:, unstriped(wb)]) / 3
    my = (y + y[:, unstriped(wa)] + y[:, unstriped(wb)]) / 3
    mgg = ((f64(guide)) ** 2 + (f64(guide)[:, unstriped(wa)]) ** 2 + (f64(guide)[:, unstriped(wb)]) ** 2) / 3
    sl = (mgy - (mg * my)) / (mgg - ((mg) ** 2) + f64(reg))
    ic = my - (sl * mg)
    return (0.5 * (sl[:, unstriped(wb)] + sl[:, unstriped(wc)])) * f64(guide) + 0.5 * (ic[:, unstriped(wb)] + ic[:, unstriped(wc)])

@@ -1,0 +1,175 @@
+import math
+from contextlib import ExitStack
+
+import concourse.mybir as mybir
+from concourse.masks import make_identity
+
+K, T, S, N = 1024, 1024, 512, 128
+FLOPS = 2 * K * S * N
+
+F32 = mybir.dt.float32
+BF16 = mybir.dt.bfloat16
+I32 = mybir.dt.int32
+U32 = mybir.dt.uint32
+U16 = mybir.dt.uint16
+U8 = mybir.dt.uint8
+FP8X4 = mybir.dt.float8_e4m3fn_x4
+ALU = mybir.AluOpType
+ACT = mybir.ActivationFunctionType
+
+P = 128
+PASSES = K // 512
+HALF = S // 2
+HALVES = [slice(0, HALF), slice(HALF, S)]
+LIST_HALVES = [slice(0, HALF // 16), slice(HALF // 16, S // 16)]
+
+
+def tile_picked_yguid_filt_p_kernel(
+    tc, x_words, x_scales, w1, guide, reg, offs, wa, wb, wc, out
+):
+    nc = tc.nc
+    with ExitStack() as ctx:
+        sb = ctx.enter_context(tc.tile_pool(name="sb", bufs=1))
+        ps = ctx.enter_context(tc.psum_pool(name="ps", bufs=1))
+
+        def row(name):
+            return sb.tile([P, S], F32, name=name)
+
+        def turned_sum(bank, terms, half):
+            for blk in range(HALF // P):
+                cols = slice(half * HALF + blk * P, half * HALF + (blk + 1) * P)
+                for n, term in enumerate(terms):
+                    nc.tensor.matmul(
+                        bank[:, blk * P : (blk + 1) * P],
+                        term[:, cols],
+                        ident[:],
+                        start=(n == 0),
+                        stop=(n == len(terms) - 1),
+                        is_transpose=True,
+                    )
+
+        offs_t = sb.tile([P, S // 16], U16)
+        wa_t = sb.tile([P, S // 16], U16)
+        wb_t = sb.tile([P, S // 16], U16)
+        wc_t = sb.tile([P, S // 16], U16)
+        g = row("g")
+        reg_t = sb.tile([P, 1], F32)
+        w_raw = sb.tile([P, PASSES, 4, N], F32)
+        words = [sb.tile([P, T], U32, name=f"words{o}") for o in range(PASSES)]
+        planes = sb.tile([P, T], U8)
+        ident = sb.tile([P, P], F32)
+        eighteen = sb.tile([P, 1], F32)
+        root = sb.tile([P, 1], F32)
+
+        nc.gpsimd.memset(planes[:].bitcast(I32), 0)
+        nc.vector.memset(eighteen[:], 18.0)
+
+        nc.sync.dma_start(offs_t[:], offs)
+        for q, queue in enumerate((nc.sync, nc.scalar, nc.sync, nc.scalar)):
+            queue.dma_start(
+                planes[32 * q : 32 * q + 4 * PASSES, :].bitcast(I32), x_scales[:, 4 * q : 4 * q + 4, :].bitcast(I32)
+            )
+        nc.scalar.dma_start(g[:], guide)
+        nc.sync.dma_start(wa_t[:], wa)
+        nc.sync.dma_start(wb_t[:], wb)
+        nc.scalar.activation(root[:], eighteen[:], ACT.Abs_reciprocal_sqrt)
+        make_identity(nc, ident[:])
+        nc.sync.dma_start(words[0][:].bitcast(I32), x_words[0].rearrange("p n t -> p (n t)").bitcast(I32))
+        nc.sync.dma_start(
+            w_raw[:].rearrange("p o j n -> p o (j n)"), w1.rearrange("(o p j) n -> p o (j n)", o=PASSES, j=4)
+        )
+        nc.sync.dma_start(words[1][:].bitcast(I32), x_words[1].rearrange("p n t -> p (n t)").bitcast(I32))
+        nc.sync.dma_start(reg_t[:], reg)
+        nc.sync.dma_start(wc_t[:], wc)
+
+        picked_scales = sb.tile([P, S], U8, align_bytes=64)
+        nc.vector.tensor_copy(picked_scales[:], planes[:].indirect(offs_t[:]))
+
+        g_plain, g3, u, v, a, b = (row(n) for n in ("g_plain", "g3", "u", "v", "a", "b"))
+        for cols in HALVES:
+            nc.scalar.copy(g_plain[:, cols], g[:, cols])
+        for dst, lst in ((u, wa_t), (v, wb_t)):
+            for cols, lc in zip(HALVES, LIST_HALVES):
+                nc.vector.tensor_tensor(dst[:, cols], g[:].indirect(lst[:, lc]), g_plain[:, cols], ALU.subtract)
+        nc.vector.scalar_tensor_tensor(a[:], u[:], 2.0, v[:], ALU.mult, ALU.subtract)
+
+        w_bf = sb.tile([P, PASSES, N, 4], BF16, align_bytes=64)
+        w_codes = sb.tile([P, PASSES * N], U32, align_bytes=64)
+        w_scales = sb.tile([P, PASSES * N], U8, align_bytes=64)
+        nc.scalar.copy(w_bf[:], w_raw[:].rearrange("p o j n -> p o n j"))
+        nc.scalar.activation(g3[:], g[:], ACT.Copy, scale=3.0)
+
+        sq_a, sq_v, den, rs, r, mean_g = (row(n) for n in ("sq_a", "sq_v", "den", "rs", "r", "mean_g"))
+        nc.scalar.activation(sq_v[:], v[:], ACT.Square, scale=1.0 / math.sqrt(6.0))
+        nc.scalar.activation(sq_a[:], a[:], ACT.Square, scale=1.0 / math.sqrt(18.0))
+        for h, cols in enumerate(HALVES):
+            bank = ps.tile([P, HALF], F32, name="bank_g", tag=f"mean{h}")
+            turned_sum(bank, (g3, u, v), h)
+            nc.scalar.activation(mean_g[:, cols], bank[:], ACT.Copy, scale=-1.0 / 3.0)
+
+        picked = [sb.tile([P, S], U32, name=f"picked{o}", align_bytes=64) for o in range(PASSES)]
+        nc.vector.tensor_copy(picked[0][:], words[0][:].indirect(offs_t[:]))
+        nc.vector.quantize_mx(w_codes[:].bitcast(FP8X4), w_scales[:], w_bf[:].rearrange("p o n j -> p (o n j)"))
+        for cols, lc in zip(HALVES, LIST_HALVES):
+            nc.vector.tensor_copy(picked[1][:, cols], words[1][:].indirect(offs_t[:, lc]))
+        y_banks = [ps.tile([P, HALF], F32, name=f"y_bank{h}", tag=f"y{h}") for h in range(2)]
+        for o in range(PASSES):
+            for h, cols in enumerate(HALVES):
+                nc.tensor.matmul_mx(
+                    y_banks[h][:],
+                    lhsT=w_codes[:, o * N : (o + 1) * N].bitcast(FP8X4),
+                    lhsT_scale=w_scales[:, o * N : (o + 1) * N],
+                    rhs=picked[o][:, cols].bitcast(FP8X4),
+                    rhs_scale=picked_scales[4 * o :, cols],
+                    start=(o == 0),
+                    stop=(o == PASSES - 1),
+                )
+        y, y_plain, y3 = row("y"), row("y_plain"), row("y3")
+        for h, cols in enumerate(HALVES):
+            nc.scalar.copy(y[:, cols], y_banks[h][:])
+            nc.scalar.copy(y_plain[:, cols], y_banks[h][:])
+        for h, cols in enumerate(HALVES):
+            nc.scalar.activation(y3[:, cols], y_banks[h][:], ACT.Copy, scale=3.0)
+
+        nc.vector.scalar_tensor_tensor(den[:], sq_a[:], reg_t[:], sq_v[:], ALU.add, ALU.add)
+        nc.vector.scalar_tensor_tensor(b[:], v[:], 2.0, u[:], ALU.mult, ALU.subtract)
+        nc.scalar.activation(rs[:], den[:], ACT.Abs_reciprocal_sqrt)
+        nc.scalar.activation(r[:], rs[:], ACT.Square, scale=root[:])
+
+        p, q, mean_y = row("p"), row("q"), row("mean_y")
+        for h, (cols, lc) in enumerate(zip(HALVES, LIST_HALVES)):
+            nc.vector.tensor_tensor(p[:, cols], y[:].indirect(wa_t[:, lc]), y_plain[:, cols], ALU.subtract)
+            nc.vector.tensor_tensor(q[:, cols], y[:].indirect(wb_t[:, lc]), y_plain[:, cols], ALU.subtract)
+            bank = ps.tile([P, HALF], F32, name="bank_y", tag=f"mean{h}")
+            turned_sum(bank, (y3, p, q), h)
+            nc.scalar.activation(mean_y[:, cols], bank[:], ACT.Copy, scale=1.0 / 6.0)
+
+        ap, bq, cov, sl = row("ap"), row("bq"), row("cov"), row("sl")
+        nc.vector.tensor_tensor(ap[:], a[:], p[:], ALU.mult)
+        for cols in HALVES:
+            nc.vector.tensor_tensor(bq[:, cols], b[:, cols], q[:, cols], ALU.mult)
+        for cols in HALVES:
+            nc.vector.tensor_tensor(cov[:, cols], ap[:, cols], bq[:, cols], ALU.add)
+        for cols in HALVES:
+            nc.vector.tensor_tensor(sl[:, cols], cov[:, cols], r[:, cols], ALU.mult)
+
+        sl_b, sl_bc, shift, ic, line, part, res = (
+            row(n) for n in ("sl_b", "sl_bc", "shift", "ic", "line", "part", "res")
+        )
+        for h, (cols, lc) in enumerate(zip(HALVES, LIST_HALVES)):
+            sl_bank = ps.tile([P, HALF], F32, name="sl_bank", tag=f"y{h}")
+            turned_sum(sl_bank, (sl,), h)
+            nc.vector.tensor_copy(sl_b[:, cols], sl[:].indirect(wb_t[:, lc]))
+            nc.vector.tensor_tensor(shift[:, cols], sl_bank[:], mean_g[:, cols], ALU.mult)
+            ic_bank = ps.tile([P, HALF], F32, name="ic_bank", tag=f"ic{h}")
+            turned_sum(ic_bank, (mean_y, shift), h)
+            nc.scalar.copy(ic[:, cols], ic_bank[:])
+        for cols, lc in zip(HALVES, LIST_HALVES):
+            nc.vector.tensor_tensor(sl_bc[:, cols], sl[:].indirect(wc_t[:, lc]), sl_b[:, cols], ALU.add)
+        for cols in HALVES:
+            nc.vector.tensor_tensor(line[:, cols], sl_bc[:, cols], g[:, cols], ALU.mult)
+        for cols, lc in zip(HALVES, LIST_HALVES):
+            nc.vector.tensor_tensor(part[:, cols], ic[:].indirect(wb_t[:, lc]), line[:, cols], ALU.add)
+        for cols, lc in zip(HALVES, LIST_HALVES):
+            nc.vector.tensor_tensor(res[:, cols], ic[:].indirect(wc_t[:, lc]), part[:, cols], ALU.add)
+            nc.sync.dma_start(out[:, cols], res[:, cols])

@@ -32,8 +32,8 @@ def tile_picked_yguid_filt_p_kernel(
         sb = ctx.enter_context(tc.tile_pool(name="sb", bufs=1))
         ps = ctx.enter_context(tc.psum_pool(name="ps", bufs=1))
 
-        def row(name):
-            return sb.tile([P, S], F32, name=name)
+        def row(name, tag=""):
+            return sb.tile([P, S], F32, name=name, tag=tag or name)
 
         def turned_sum(bank, terms, half):
             for blk in range(HALF // P):
@@ -54,67 +54,57 @@ def tile_picked_yguid_filt_p_kernel(
         wc_t = sb.tile([P, S // 16], U16)
         g = row("g")
         reg_t = sb.tile([P, 1], F32)
-        w_raw = sb.tile([P, PASSES, 4, N], F32)
-        words = [sb.tile([P, T], U32, name=f"words{o}") for o in range(PASSES)]
+        w_raw = sb.tile([P, PASSES, 4, N], F32, tag="w_raw")
+        words = [sb.tile([P, T], U32, name=f"words{o}", tag=f"words{o}") for o in range(PASSES)]
         planes = sb.tile([P, T], U8)
         ident = sb.tile([P, P], F32)
         eighteen = sb.tile([P, 1], F32)
         root = sb.tile([P, 1], F32)
 
         nc.gpsimd.memset(planes[:].bitcast(I32), 0)
-        nc.vector.memset(eighteen[:], 18.0)
+        nc.gpsimd.memset(eighteen[:], 18.0)
 
         nc.sync.dma_start(offs_t[:], offs)
-        for q, queue in enumerate((nc.sync, nc.scalar, nc.sync, nc.scalar)):
+        for quad, queue in enumerate((nc.sync, nc.scalar, nc.sync, nc.scalar)):
             queue.dma_start(
-                planes[32 * q : 32 * q + 4 * PASSES, :].bitcast(I32), x_scales[:, 4 * q : 4 * q + 4, :].bitcast(I32)
+                planes[32 * quad : 32 * quad + 4 * PASSES, :].bitcast(I32),
+                x_scales[:, 4 * quad : 4 * quad + 4, :].bitcast(I32),
             )
-        nc.scalar.dma_start(g[:], guide)
-        nc.sync.dma_start(wa_t[:], wa)
-        nc.sync.dma_start(wb_t[:], wb)
         nc.scalar.activation(root[:], eighteen[:], ACT.Abs_reciprocal_sqrt)
         make_identity(nc, ident[:])
-        nc.sync.dma_start(words[0][:].bitcast(I32), x_words[0].rearrange("p n t -> p (n t)").bitcast(I32))
+        x_rows = [x_words[o].rearrange("p n t -> p (n t)").bitcast(I32) for o in range(PASSES)]
+        nc.sync.dma_start(words[0][:].bitcast(I32), x_rows[0])
+        nc.sync.dma_start(g[:], guide)
+        nc.sync.dma_start(wa_t[:], wa)
         nc.sync.dma_start(
             w_raw[:].rearrange("p o j n -> p o (j n)"), w1.rearrange("(o p j) n -> p o (j n)", o=PASSES, j=4)
         )
-        nc.sync.dma_start(words[1][:].bitcast(I32), x_words[1].rearrange("p n t -> p (n t)").bitcast(I32))
+        nc.sync.dma_start(words[1][:].bitcast(I32), x_rows[1])
+        nc.sync.dma_start(wb_t[:], wb)
         nc.sync.dma_start(reg_t[:], reg)
         nc.sync.dma_start(wc_t[:], wc)
 
+        picked = [sb.tile([P, S], U32, name=f"picked{o}", align_bytes=64) for o in range(PASSES)]
         picked_scales = sb.tile([P, S], U8, align_bytes=64)
         nc.vector.tensor_copy(picked_scales[:], planes[:].indirect(offs_t[:]))
+        nc.vector.tensor_copy(picked[0][:], words[0][:].indirect(offs_t[:]))
 
-        g_plain, g3, u, v, a, b = (row(n) for n in ("g_plain", "g3", "u", "v", "a", "b"))
+        g_plain, g3, u, a, b = (row(n) for n in ("g_plain", "g3", "u", "a", "b"))
         for cols in HALVES:
             nc.scalar.copy(g_plain[:, cols], g[:, cols])
-        for dst, lst in ((u, wa_t), (v, wb_t)):
-            for cols, lc in zip(HALVES, LIST_HALVES):
-                nc.vector.tensor_tensor(dst[:, cols], g[:].indirect(lst[:, lc]), g_plain[:, cols], ALU.subtract)
-        nc.vector.scalar_tensor_tensor(a[:], u[:], 2.0, v[:], ALU.mult, ALU.subtract)
+        for cols, lc in zip(HALVES, LIST_HALVES):
+            nc.vector.tensor_tensor(u[:, cols], g[:].indirect(wa_t[:, lc]), g_plain[:, cols], ALU.subtract)
 
         w_bf = sb.tile([P, PASSES, N, 4], BF16, align_bytes=64)
         w_codes = sb.tile([P, PASSES * N], U32, align_bytes=64)
         w_scales = sb.tile([P, PASSES * N], U8, align_bytes=64)
         nc.scalar.copy(w_bf[:], w_raw[:].rearrange("p o j n -> p o n j"))
-        nc.scalar.activation(g3[:], g[:], ACT.Copy, scale=3.0)
-
-        sq_a, sq_v, den, rs, r, mean_g = (row(n) for n in ("sq_a", "sq_v", "den", "rs", "r", "mean_g"))
-        nc.scalar.activation(sq_v[:], v[:], ACT.Square, scale=1.0 / math.sqrt(6.0))
-        nc.scalar.activation(sq_a[:], a[:], ACT.Square, scale=1.0 / math.sqrt(18.0))
-        for h, cols in enumerate(HALVES):
-            bank = ps.tile([P, HALF], F32, name="bank_g", tag=f"mean{h}")
-            turned_sum(bank, (g3, u, v), h)
-            nc.scalar.activation(mean_g[:, cols], bank[:], ACT.Copy, scale=-1.0 / 3.0)
-
-        picked = [sb.tile([P, S], U32, name=f"picked{o}", align_bytes=64) for o in range(PASSES)]
-        nc.vector.tensor_copy(picked[0][:], words[0][:].indirect(offs_t[:]))
+        nc.vector.tensor_copy(picked[1][:], words[1][:].indirect(offs_t[:]))
         nc.vector.quantize_mx(w_codes[:].bitcast(FP8X4), w_scales[:], w_bf[:].rearrange("p o n j -> p (o n j)"))
-        for cols, lc in zip(HALVES, LIST_HALVES):
-            nc.vector.tensor_copy(picked[1][:, cols], words[1][:].indirect(offs_t[:, lc]))
+        y, y_plain, y3 = row("y"), row("y_plain"), row("y3")
         y_banks = [ps.tile([P, HALF], F32, name=f"y_bank{h}", tag=f"y{h}") for h in range(2)]
-        for o in range(PASSES):
-            for h, cols in enumerate(HALVES):
+        for h, cols in enumerate(HALVES):
+            for o in range(PASSES):
                 nc.tensor.matmul_mx(
                     y_banks[h][:],
                     lhsT=w_codes[:, o * N : (o + 1) * N].bitcast(FP8X4),
@@ -124,17 +114,37 @@ def tile_picked_yguid_filt_p_kernel(
                     start=(o == 0),
                     stop=(o == PASSES - 1),
                 )
-        y, y_plain, y3 = row("y"), row("y_plain"), row("y3")
-        for h, cols in enumerate(HALVES):
             nc.scalar.copy(y[:, cols], y_banks[h][:])
             nc.scalar.copy(y_plain[:, cols], y_banks[h][:])
+
+        sq_b, floor, rs, r, mean_g = (row(n) for n in ("sq_b", "floor", "rs", "r", "mean_g"))
+        sq_u = row("sq_u", tag="w_raw")
+        nc.scalar.activation(g3[:], g[:], ACT.Copy, scale=3.0)
+        nc.scalar.activation(sq_u[:], u[:], ACT.Square, scale=1.0 / math.sqrt(6.0))
+        nc.scalar.activation(floor[:], sq_u[:], ACT.Identity, bias=reg_t[:])
+
+        v = row("v", tag="words1")
+        for cols, lc in zip(HALVES, LIST_HALVES):
+            nc.vector.tensor_tensor(v[:, cols], g[:].indirect(wb_t[:, lc]), g_plain[:, cols], ALU.subtract)
+        for cols in HALVES:
+            nc.vector.scalar_tensor_tensor(b[:, cols], v[:, cols], 2.0, u[:, cols], ALU.mult, ALU.subtract)
+        nc.vector.scalar_tensor_tensor(a[:], u[:], 2.0, v[:], ALU.mult, ALU.subtract)
+        for cols in HALVES:
+            nc.scalar.activation(sq_b[:, cols], b[:, cols], ACT.Square, scale=1.0 / math.sqrt(18.0))
+        r_banks = []
+        for h, cols in enumerate(HALVES):
+            bank = ps.tile([P, HALF], F32, name="bank_den", tag=f"den{h}")
+            turned_sum(bank, (floor, sq_b), h)
+            nc.scalar.activation(rs[:, cols], bank[:], ACT.Abs_reciprocal_sqrt)
+            nc.scalar.activation(r[:, cols], rs[:, cols], ACT.Square, scale=root[:])
+            r_banks.append(ps.tile([P, HALF], F32, name="bank_r", tag=f"ic{h}"))
+            turned_sum(r_banks[h], (r,), h)
         for h, cols in enumerate(HALVES):
             nc.scalar.activation(y3[:, cols], y_banks[h][:], ACT.Copy, scale=3.0)
-
-        nc.vector.scalar_tensor_tensor(den[:], sq_a[:], reg_t[:], sq_v[:], ALU.add, ALU.add)
-        nc.vector.scalar_tensor_tensor(b[:], v[:], 2.0, u[:], ALU.mult, ALU.subtract)
-        nc.scalar.activation(rs[:], den[:], ACT.Abs_reciprocal_sqrt)
-        nc.scalar.activation(r[:], rs[:], ACT.Square, scale=root[:])
+        for h, cols in enumerate(HALVES):
+            bank = ps.tile([P, HALF], F32, name="bank_g", tag=f"mean{h}")
+            turned_sum(bank, (g3, u, v), h)
+            nc.scalar.activation(mean_g[:, cols], bank[:], ACT.Copy, scale=-1.0 / 3.0)
 
         p, q, mean_y = row("p"), row("q"), row("mean_y")
         for h, (cols, lc) in enumerate(zip(HALVES, LIST_HALVES)):
@@ -150,8 +160,8 @@ def tile_picked_yguid_filt_p_kernel(
             nc.vector.tensor_tensor(bq[:, cols], b[:, cols], q[:, cols], ALU.mult)
         for cols in HALVES:
             nc.vector.tensor_tensor(cov[:, cols], ap[:, cols], bq[:, cols], ALU.add)
-        for cols in HALVES:
-            nc.vector.tensor_tensor(sl[:, cols], cov[:, cols], r[:, cols], ALU.mult)
+        for h, cols in enumerate(HALVES):
+            nc.vector.tensor_tensor(sl[:, cols], r_banks[h][:], cov[:, cols], ALU.mult)
 
         sl_b, sl_bc, shift, ic, line, part, res = (
             row(n) for n in ("sl_b", "sl_bc", "shift", "ic", "line", "part", "res")
@@ -159,17 +169,20 @@ def tile_picked_yguid_filt_p_kernel(
         for h, (cols, lc) in enumerate(zip(HALVES, LIST_HALVES)):
             sl_bank = ps.tile([P, HALF], F32, name="sl_bank", tag=f"y{h}")
             turned_sum(sl_bank, (sl,), h)
-            nc.vector.tensor_copy(sl_b[:, cols], sl[:].indirect(wb_t[:, lc]))
             nc.vector.tensor_tensor(shift[:, cols], sl_bank[:], mean_g[:, cols], ALU.mult)
             ic_bank = ps.tile([P, HALF], F32, name="ic_bank", tag=f"ic{h}")
             turned_sum(ic_bank, (mean_y, shift), h)
             nc.scalar.copy(ic[:, cols], ic_bank[:])
-        for cols, lc in zip(HALVES, LIST_HALVES):
-            nc.vector.tensor_tensor(sl_bc[:, cols], sl[:].indirect(wc_t[:, lc]), sl_b[:, cols], ALU.add)
+        sl_b_halves = [sl_b[:, HALVES[0]], mean_g[:, HALVES[1]]]
+        for dst, lc in zip(sl_b_halves, LIST_HALVES):
+            nc.vector.tensor_copy(dst, sl[:].indirect(wb_t[:, lc]))
+        for src, cols, lc in zip(sl_b_halves, HALVES, LIST_HALVES):
+            nc.vector.tensor_tensor(sl_bc[:, cols], sl[:].indirect(wc_t[:, lc]), src, ALU.add)
         for cols in HALVES:
             nc.vector.tensor_tensor(line[:, cols], sl_bc[:, cols], g[:, cols], ALU.mult)
         for cols, lc in zip(HALVES, LIST_HALVES):
             nc.vector.tensor_tensor(part[:, cols], ic[:].indirect(wb_t[:, lc]), line[:, cols], ALU.add)
-        for cols, lc in zip(HALVES, LIST_HALVES):
+        for lo, hi in ((0, HALF), (HALF, S - P), (S - P, S)):
+            cols, lc = slice(lo, hi), slice(lo // 16, hi // 16)
             nc.vector.tensor_tensor(res[:, cols], ic[:].indirect(wc_t[:, lc]), part[:, cols], ALU.add)
             nc.sync.dma_start(out[:, cols], res[:, cols])

import math
from contextlib import ExitStack

import concourse.mybir as mybir
from concourse.masks import make_identity

K, T, S, N = 1024, 1024, 512, 128
FLOPS = 2 * K * S * N

F32 = mybir.dt.float32
BF16 = mybir.dt.bfloat16
I32 = mybir.dt.int32
U32 = mybir.dt.uint32
U16 = mybir.dt.uint16
U8 = mybir.dt.uint8
FP8X4 = mybir.dt.float8_e4m3fn_x4
ALU = mybir.AluOpType
ACT = mybir.ActivationFunctionType

P = 128
PASSES = K // 512
HALF = S // 2
HALVES = [slice(0, HALF), slice(HALF, S)]
LIST_HALVES = [slice(0, HALF // 16), slice(HALF // 16, S // 16)]


def tile_picked_yguid_filt_p_kernel(
    tc, x_words, x_scales, w1, guide, reg, offs, wa, wb, wc, out
):
    nc = tc.nc
    with ExitStack() as ctx:
        sb = ctx.enter_context(tc.tile_pool(name="sb", bufs=1))
        ps = ctx.enter_context(tc.psum_pool(name="ps", bufs=1))

        def row(name, tag=""):
            return sb.tile([P, S], F32, name=name, tag=tag or name)

        def turned_sum(bank, terms, half):
            for blk in range(HALF // P):
                cols = slice(half * HALF + blk * P, half * HALF + (blk + 1) * P)
                for n, term in enumerate(terms):
                    nc.tensor.matmul(
                        bank[:, blk * P : (blk + 1) * P],
                        term[:, cols],
                        ident[:],
                        start=(n == 0),
                        stop=(n == len(terms) - 1),
                        is_transpose=True,
                    )

        offs_t = sb.tile([P, S // 16], U16)
        wa_t = sb.tile([P, S // 16], U16)
        wb_t = sb.tile([P, S // 16], U16)
        wc_t = sb.tile([P, S // 16], U16)
        g = row("g")
        reg_t = sb.tile([P, 1], F32)
        w_raw = sb.tile([P, PASSES, 4, N], F32, tag="w_raw")
        words = [sb.tile([P, T], U32, name=f"words{o}", tag=f"words{o}") for o in range(PASSES)]
        planes = sb.tile([P, T], U8)
        ident = sb.tile([P, P], F32)
        eighteen = sb.tile([P, 1], F32)
        root = sb.tile([P, 1], F32)

        nc.gpsimd.memset(planes[:].bitcast(I32), 0)
        nc.gpsimd.memset(eighteen[:], 18.0)

        nc.sync.dma_start(offs_t[:], offs)
        for quad, queue in enumerate((nc.sync, nc.scalar, nc.sync, nc.scalar)):
            queue.dma_start(
                planes[32 * quad : 32 * quad + 4 * PASSES, :].bitcast(I32),
                x_scales[:, 4 * quad : 4 * quad + 4, :].bitcast(I32),
            )
        nc.scalar.activation(root[:], eighteen[:], ACT.Abs_reciprocal_sqrt)
        make_identity(nc, ident[:])
        x_rows = [x_words[o].rearrange("p n t -> p (n t)").bitcast(I32) for o in range(PASSES)]
        nc.sync.dma_start(words[0][:].bitcast(I32), x_rows[0])
        nc.sync.dma_start(g[:], guide)
        nc.sync.dma_start(wa_t[:], wa)
        nc.sync.dma_start(
            w_raw[:].rearrange("p o j n -> p o (j n)"), w1.rearrange("(o p j) n -> p o (j n)", o=PASSES, j=4)
        )
        nc.sync.dma_start(words[1][:].bitcast(I32), x_rows[1])
        nc.sync.dma_start(wb_t[:], wb)
        nc.sync.dma_start(reg_t[:], reg)
        nc.sync.dma_start(wc_t[:], wc)

        picked = [sb.tile([P, S], U32, name=f"picked{o}", align_bytes=64) for o in range(PASSES)]
        picked_scales = sb.tile([P, S], U8, align_bytes=64)
        nc.vector.tensor_copy(picked_scales[:], planes[:].indirect(offs_t[:]))
        nc.vector.tensor_copy(picked[0][:], words[0][:].indirect(offs_t[:]))

        g_plain, g3, u, a, b = (row(n) for n in ("g_plain", "g3", "u", "a", "b"))
        for cols in HALVES:
            nc.scalar.copy(g_plain[:, cols], g[:, cols])
        for cols, lc in zip(HALVES, LIST_HALVES):
            nc.vector.tensor_tensor(u[:, cols], g[:].indirect(wa_t[:, lc]), g_plain[:, cols], ALU.subtract)

        w_bf = sb.tile([P, PASSES, N, 4], BF16, align_bytes=64)
        w_codes = sb.tile([P, PASSES * N], U32, align_bytes=64)
        w_scales = sb.tile([P, PASSES * N], U8, align_bytes=64)
        nc.scalar.copy(w_bf[:], w_raw[:].rearrange("p o j n -> p o n j"))
        nc.vector.tensor_copy(picked[1][:], words[1][:].indirect(offs_t[:]))
        nc.vector.quantize_mx(w_codes[:].bitcast(FP8X4), w_scales[:], w_bf[:].rearrange("p o n j -> p (o n j)"))
        y, y_plain, y3 = row("y"), row("y_plain"), row("y3")
        y_banks = [ps.tile([P, HALF], F32, name=f"y_bank{h}", tag=f"y{h}") for h in range(2)]
        for h, cols in enumerate(HALVES):
            for o in range(PASSES):
                nc.tensor.matmul_mx(
                    y_banks[h][:],
                    lhsT=w_codes[:, o * N : (o + 1) * N].bitcast(FP8X4),
                    lhsT_scale=w_scales[:, o * N : (o + 1) * N],
                    rhs=picked[o][:, cols].bitcast(FP8X4),
                    rhs_scale=picked_scales[4 * o :, cols],
                    start=(o == 0),
                    stop=(o == PASSES - 1),
                )
            nc.scalar.copy(y[:, cols], y_banks[h][:])
            nc.scalar.copy(y_plain[:, cols], y_banks[h][:])

        sq_b, floor, rs, r, mean_g = (row(n) for n in ("sq_b", "floor", "rs", "r", "mean_g"))
        sq_u = row("sq_u", tag="w_raw")
        nc.scalar.activation(g3[:], g[:], ACT.Copy, scale=3.0)
        nc.scalar.activation(sq_u[:], u[:], ACT.Square, scale=1.0 / math.sqrt(6.0))
        nc.scalar.activation(floor[:], sq_u[:], ACT.Identity, bias=reg_t[:])

        v = row("v", tag="words1")
        for cols, lc in zip(HALVES, LIST_HALVES):
            nc.vector.tensor_tensor(v[:, cols], g[:].indirect(wb_t[:, lc]), g_plain[:, cols], ALU.subtract)
        for cols in HALVES:
            nc.vector.scalar_tensor_tensor(b[:, cols], v[:, cols], 2.0, u[:, cols], ALU.mult, ALU.subtract)
        nc.vector.scalar_tensor_tensor(a[:], u[:], 2.0, v[:], ALU.mult, ALU.subtract)
        for cols in HALVES:
            nc.scalar.activation(sq_b[:, cols], b[:, cols], ACT.Square, scale=1.0 / math.sqrt(18.0))
        r_banks = []
        for h, cols in enumerate(HALVES):
            bank = ps.tile([P, HALF], F32, name="bank_den", tag=f"den{h}")
            turned_sum(bank, (floor, sq_b), h)
            nc.scalar.activation(rs[:, cols], bank[:], ACT.Abs_reciprocal_sqrt)
            nc.scalar.activation(r[:, cols], rs[:, cols], ACT.Square, scale=root[:])
            r_banks.append(ps.tile([P, HALF], F32, name="bank_r", tag=f"ic{h}"))
            turned_sum(r_banks[h], (r,), h)
        for h, cols in enumerate(HALVES):
            nc.scalar.activation(y3[:, cols], y_banks[h][:], ACT.Copy, scale=3.0)
        for h, cols in enumerate(HALVES):
            bank = ps.tile([P, HALF], F32, name="bank_g", tag=f"mean{h}")
            turned_sum(bank, (g3, u, v), h)
            nc.scalar.activation(mean_g[:, cols], bank[:], ACT.Copy, scale=-1.0 / 3.0)

        p, q, mean_y = row("p"), row("q"), row("mean_y")
        for h, (cols, lc) in enumerate(zip(HALVES, LIST_HALVES)):
            nc.vector.tensor_tensor(p[:, cols], y[:].indirect(wa_t[:, lc]), y_plain[:, cols], ALU.subtract)
            nc.vector.tensor_tensor(q[:, cols], y[:].indirect(wb_t[:, lc]), y_plain[:, cols], ALU.subtract)
            bank = ps.tile([P, HALF], F32, name="bank_y", tag=f"mean{h}")
            turned_sum(bank, (y3, p, q), h)
            nc.scalar.activation(mean_y[:, cols], bank[:], ACT.Copy, scale=1.0 / 6.0)

        ap, bq, cov, sl = row("ap"), row("bq"), row("cov"), row("sl")
        nc.vector.tensor_tensor(ap[:], a[:], p[:], ALU.mult)
        for cols in HALVES:
            nc.vector.tensor_tensor(bq[:, cols], b[:, cols], q[:, cols], ALU.mult)
        for cols in HALVES:
            nc.vector.tensor_tensor(cov[:, cols], ap[:, cols], bq[:, cols], ALU.add)
        for h, cols in enumerate(HALVES):
            nc.vector.tensor_tensor(sl[:, cols], r_banks[h][:], cov[:, cols], ALU.mult)

        sl_b, sl_bc, shift, ic, line, part, res = (
            row(n) for n in ("sl_b", "sl_bc", "shift", "ic", "line", "part", "res")
        )
        for h, (cols, lc) in enumerate(zip(HALVES, LIST_HALVES)):
            sl_bank = ps.tile([P, HALF], F32, name="sl_bank", tag=f"y{h}")
            turned_sum(sl_bank, (sl,), h)
            nc.vector.tensor_tensor(shift[:, cols], sl_bank[:], mean_g[:, cols], ALU.mult)
            ic_bank = ps.tile([P, HALF], F32, name="ic_bank", tag=f"ic{h}")
            turned_sum(ic_bank, (mean_y, shift), h)
            nc.scalar.copy(ic[:, cols], ic_bank[:])
        sl_b_halves = [sl_b[:, HALVES[0]], mean_g[:, HALVES[1]]]
        for dst, lc in zip(sl_b_halves, LIST_HALVES):
            nc.vector.tensor_copy(dst, sl[:].indirect(wb_t[:, lc]))
        for src, cols, lc in zip(sl_b_halves, HALVES, LIST_HALVES):
            nc.vector.tensor_tensor(sl_bc[:, cols], sl[:].indirect(wc_t[:, lc]), src, ALU.add)
        for cols in HALVES:
            nc.vector.tensor_tensor(line[:, cols], sl_bc[:, cols], g[:, cols], ALU.mult)
        for cols, lc in zip(HALVES, LIST_HALVES):
            nc.vector.tensor_tensor(part[:, cols], ic[:].indirect(wb_t[:, lc]), line[:, cols], ALU.add)
        for lo, hi in ((0, HALF), (HALF, S - P), (S - P, S)):
            cols, lc = slice(lo, hi), slice(lo // 16, hi // 16)
            nc.vector.tensor_tensor(res[:, cols], ic[:].indirect(wc_t[:, lc]), part[:, cols], ALU.add)
            nc.sync.dma_start(out[:, cols], res[:, cols])
